import numpy as np
import ml_dtypes


def mxq(x, axis, fmt="e4m3"):
    dtype, down = {"e4m3": (ml_dtypes.float8_e4m3fn, 7), "e5m2": (ml_dtypes.float8_e5m2, 14)}[fmt]
    v = np.moveaxis(np.asarray(x, np.float32).astype(ml_dtypes.bfloat16).astype(np.float64), axis, -1)
    blocks = v.reshape(v.shape[:-1] + (-1, 32))
    amax = np.abs(blocks).max(-1, keepdims=True)
    byte = np.maximum(np.where(amax > 0, np.frexp(amax)[1] - 1 + 127, 0) - down, 1)
    scale = np.exp2(byte - 127.0)
    codes = (blocks / scale).astype(np.float32).astype(dtype).astype(np.float64)
    return np.moveaxis((codes * scale).reshape(v.shape), -1, axis)


WIDE = False


def mx_kscale(k):
    if not WIDE:
        return np.ones(k)
    levels = np.array([30, -30])
    if k % 512:
        return np.exp2(np.random.permutation(np.resize(levels, k // 32))).repeat(32)
    a = np.empty((k // 512, 16))
    for p in range(k // 512):
        a[p, :8] = np.random.permutation(np.resize(levels, 8))
        for g in range(8):
            far = levels[np.abs(levels - a[p, g]) >= 10]
            a[p, g + 8] = far[np.random.randint(len(far))]
    return np.exp2(a.ravel()).repeat(32)


def f64(x):
    return np.asarray(x).astype(np.float64)


def striped(idx):
    return np.tile(np.asarray(idx).reshape(-1, 16).T, (8, 1)).astype(np.uint16)


def unstriped(offs):
    return offs[:16].T.reshape(-1).astype(np.int64)


E2M1 = np.array([0.0, 0.5, 1.0, 1.5, 2.0, 3.0, 4.0, 6.0, -0.0, -0.5, -1.0, -1.5, -2.0, -3.0, -4.0, -6.0])


def pack_weight(w, fmt):
    k, n = w.shape
    w = f64(np.asarray(w, np.float32).astype(ml_dtypes.bfloat16)).reshape(k // 32, 32, n)
    amax = np.abs(w).max(1)
    if fmt in ("e4m3", "e5m2"):
        byte = np.frexp(amax)[1] - 1 + 127 - (7 if fmt == "e4m3" else 14)
    else:
        mant, ex = np.frexp(amax / 6.0)
        byte = np.where(mant > 0.5, ex, ex - 1) + 127
    byte = np.clip(np.where(amax > 0, byte, 1), 1, 254)
    scaled = (w * np.exp2(127.0 - byte)[:, None, :]).reshape(k, n).astype(np.float32)
    by_word = np.ascontiguousarray(scaled.reshape(k // 512, 128, 4, n).transpose(0, 1, 3, 2))
    if fmt in ("e4m3", "e5m2"):
        words = by_word.astype(ml_dtypes.float8_e4m3fn if fmt == "e4m3" else ml_dtypes.float8_e5m2).view(np.uint8)
    else:
        c = by_word.astype(ml_dtypes.float4_e2m1fn).view(np.uint8) & 0xF
        words = (c[..., 0::2] | (c[..., 1::2] << 4)).reshape(k // 512, 128, 2 * n)
    return np.ascontiguousarray(words), np.ascontiguousarray(byte.astype(np.uint8).reshape(k // 512, 16, n))


def unpack_weight(words, scales, fmt):
    g, _, n = scales.shape
    words = np.ascontiguousarray(words).reshape(g, 128, n, -1)
    if fmt in ("e4m3", "e5m2"):
        vals = words.view(ml_dtypes.float8_e4m3fn if fmt == "e4m3" else ml_dtypes.float8_e5m2).astype(np.float64)
    else:
        nib = np.empty((g, 128, n, 4), np.uint8)
        nib[..., 0::2] = words & 0xF
        nib[..., 1::2] = words >> 4
        vals = E2M1[nib]
    vals = vals * np.repeat(np.exp2(scales.astype(np.float64) - 127.0), 8, axis=1)[..., None]
    return vals.transpose(0, 1, 3, 2).reshape(g * 512, n)


K, T, I, J, N, Z, S, V, C = 512, 1024, 512, 256, 256, 1024, 1024, 1024, 512


def setup_inputs():
    n = np.random.standard_normal
    idx = np.random.permutation(T)[:I]
    idx2 = np.random.permutation(Z)[:J]
    idx3 = np.random.permutation(V)[:J]
    idx4 = np.random.permutation(C)[:J]
    idx5 = np.random.permutation(C)[:J]
    idx6 = np.random.permutation(S)[:N]
    fk = mx_kscale(K)
    fi = mx_kscale(I)
    ti = np.ones(T)
    ti[idx] = fi
    xkp = pack_weight(n((K, T)) * 0.3 * fk[:, None] * ti, "e4m3")
    xqp = pack_weight(n((K, Z)) * 0.3 / fk[:, None], "e2m1")
    xrp = pack_weight(n((K, V)) * 0.3 / fk[:, None], "e5m2")
    vsp = pack_weight(n((I, S)) / fi[:, None], "e2m1")
    return {
        "xk_words": xkp[0],
        "xk_scales": xkp[1],
        "xq_words": xqp[0],
        "xq_scales": xqp[1],
        "xr_words": xrp[0],
        "xr_scales": xrp[1],
        "vs_words": vsp[0],
        "vs_scales": vsp[1],
        "offs": striped(idx),
        "offs2": striped(idx2),
        "offs3": striped(idx3),
        "offs4": striped(idx4),
        "offs5": striped(idx5),
        "offs6": striped(idx6),
    }


def reference(xk_words, xk_scales, xq_words, xq_scales, xr_words, xr_scales, vs_words, vs_scales, offs, offs2, offs3, offs4, offs5, offs6):
    idx = unstriped(offs)
    idx2 = unstriped(offs2)
    idx3 = unstriped(offs3)
    idx4 = unstriped(offs4)
    idx5 = unstriped(offs5)
    idx6 = unstriped(offs6)
    xku = unpack_weight(xk_words, xk_scales, "e4m3")
    xqu = unpack_weight(xq_words, xq_scales, "e2m1")
    xru = unpack_weight(xr_words, xr_scales, "e5m2")
    vsu = unpack_weight(vs_words, vs_scales, "e2m1")
    xkidxg = xku[:, idx]
    xqidx2g = xqu[:, idx2]
    s1 = xkidxg.T @ xqidx2g
    xridx3g = xru[:, idx3]
    s2 = xkidxg.T @ xridx3g
    pw = np.zeros((I, C))
    pw[:, idx4] = s1
    hid = np.maximum(pw[:, idx5], s2)
    vsidx6g = vsu[:, idx6]
    hidq = mxq(hid, 0, "e4m3")
    y = vsidx6g.T @ hidq
    return y

@@ -1,0 +1,162 @@
+from contextlib import ExitStack
+
+import concourse.mybir as mybir
+
+K, T, I, J, N, C = 512, 1024, 512, 256, 256, 512
+FLOPS = 2 * K * I * J * 2 + 2 * I * N * J
+
+F32 = mybir.dt.float32
+BF16 = mybir.dt.bfloat16
+I32 = mybir.dt.int32
+U32 = mybir.dt.uint32
+U16 = mybir.dt.uint16
+U8 = mybir.dt.uint8
+E4M3 = mybir.dt.float8_e4m3fn_x4
+E5M2 = mybir.dt.float8_e5m2_x4
+E2M1 = mybir.dt.float4_e2m1fn_x4
+COPY = mybir.ActivationFunctionType.Copy
+MAX = mybir.AluOpType.max
+
+P = 128
+PACK = 4
+HALF = J // 2
+
+
+def tile_list_contest_rivals_board_plain_kernel(
+    tc, xk_words, xk_scales, xq_words, xq_scales, xr_words, xr_scales, vs_words, vs_scales,
+    offs, offs2, offs3, offs4, offs5, offs6, out,
+):
+    nc = tc.nc
+    with ExitStack() as ctx:
+        sb = ctx.enter_context(tc.tile_pool(name="sb", bufs=1))
+        ps = ctx.enter_context(tc.psum_pool(name="ps", bufs=1))
+
+        def sbuf(name, cols, dtype):
+            return sb.tile([P, cols], dtype, name=name, align_bytes=64)
+
+        def load_list(name, src):
+            tile = sb.tile(list(src.shape), U16, name=name)
+            nc.sync.dma_start(tile[:], src)
+            return tile
+
+        def load_words(name, src, dtype):
+            tile = sbuf(name, T, dtype)
+            nc.sync.dma_start(tile[:].bitcast(I32), src.bitcast(I32))
+            return tile
+
+        def zeroed_plane(name):
+            tile = sbuf(name, T, U8)
+            nc.vector.memset(tile[:].bitcast(I32), 0)
+            return tile
+
+        def load_scales(queue, tile, src):
+            for q in range(4):
+                queue.dma_start(tile[32 * q : 32 * q + 4, :].bitcast(I32), src[0, 4 * q : 4 * q + 4, :].bitcast(I32))
+
+        k_plane = zeroed_plane("k_plane")
+        q_plane = zeroed_plane("q_plane")
+        r_plane = zeroed_plane("r_plane")
+        v_plane = zeroed_plane("v_plane")
+        board = []
+        for t in range(PACK):
+            tile = sbuf("board%d" % t, C, F32)
+            nc.vector.memset(tile[:], 0.0)
+            board.append(tile)
+
+        q_list = load_list("q_list", offs2)
+        q_table = load_words("q_table", xq_words[0], U16)
+        k_list = load_list("k_list", offs)
+        k_table = load_words("k_table", xk_words[0].rearrange("p n t -> p (n t)"), U32)
+        load_scales(nc.scalar, k_plane, xk_scales)
+        load_scales(nc.scalar, q_plane, xq_scales)
+        r_list = load_list("r_list", offs3)
+        put_list = load_list("put_list", offs4)
+        r_table = load_words("r_table", xr_words[0].rearrange("p n t -> p (n t)"), U32)
+        v_table = load_words("v_table", vs_words[0], U16)
+        load_scales(nc.sync, r_plane, xr_scales)
+        v_list = load_list("v_list", offs6)
+        get_list = load_list("get_list", offs5)
+        load_scales(nc.sync, v_plane, vs_scales)
+
+        def gather(name, table, lst, count, dtype):
+            tile = sbuf(name, count, dtype)
+            nc.vector.tensor_copy(tile[:], table[:].indirect(lst[:]))
+            return tile
+
+        def gather_dealt(name, table, lst, dtype):
+            tile = sbuf(name, I, dtype)
+            nc.vector.tensor_copy(tile[:].rearrange("p (t m) -> p m t", t=PACK), table[:].indirect(lst[:]))
+            return tile
+
+        q_words = gather("q_words", q_table, q_list, J, U16)
+        k_scales = gather_dealt("k_scales", k_plane, k_list, U8)
+        k_words = gather_dealt("k_words", k_table, k_list, U32)
+        q_scales = gather("q_scales", q_plane, q_list, J, U8)
+
+        def keys(t):
+            cols = slice(t * P, (t + 1) * P)
+            return dict(lhsT=k_words[:, cols].bitcast(E4M3), lhsT_scale=k_scales[:, cols])
+
+        s1_bank0 = ps.tile([P, J], F32, name="s1_bank0")
+        s1_bank1 = ps.tile([P, J], F32, name="s1_bank1")
+        s1_bank23 = ps.tile([P, 2 * J], F32, name="s1_bank23")
+        s1_psum = [s1_bank0[:], s1_bank1[:], s1_bank23[:, 0:J], s1_bank23[:, J : 2 * J]]
+        for t in range(PACK):
+            nc.tensor.matmul_mx(out=s1_psum[t], rhs=q_words[:].bitcast(E2M1), rhs_scale=q_scales[:],
+                                start=True, stop=True, **keys(t))
+
+        s1_0 = sbuf("s1_0", J, F32)
+        s1_1 = sbuf("s1_1", J, F32)
+        s1_23 = sbuf("s1_23", 2 * J, F32)
+        picked = sb.tile([P, PACK, J], F32, name="picked", align_bytes=64)
+
+        nc.scalar.copy(s1_0[:], s1_bank0[:])
+        nc.scalar.activation(board[0][:].indirect(put_list[:]), s1_0[:], COPY)
+
+        r_words = gather("r_words", r_table, r_list, J, U32)
+        nc.vector.tensor_copy(s1_1[:], s1_bank1[:])
+        nc.vector.tensor_copy(board[1][:].indirect(put_list[:]), s1_1[:])
+
+        nc.scalar.copy(s1_23[:], s1_bank23[:])
+        nc.scalar.activation(board[2][:].indirect(put_list[:]), s1_23[:, 0:J], COPY)
+        nc.scalar.activation(board[3][:].indirect(put_list[:]), s1_23[:, J : 2 * J], COPY)
+
+        r_scales = gather("r_scales", r_plane, r_list, J, U8)
+        s2_banks = [ps.tile([P, PACK, HALF], F32, name="s2_bank%d" % h) for h in range(2)]
+        for h in range(2):
+            cols = slice(h * HALF, (h + 1) * HALF)
+            for t in range(PACK):
+                nc.tensor.matmul_mx(out=s2_banks[h][:, t, :], rhs=r_words[:, cols].bitcast(E5M2),
+                                    rhs_scale=r_scales[:, cols], start=True, stop=True, **keys(t))
+
+        v_words = gather("v_words", v_table, v_list, N, U16)
+        v_scales = gather("v_scales", v_plane, v_list, N, U8)
+
+        for t in range(3):
+            nc.vector.tensor_copy(picked[:, t, :], board[t][:].indirect(get_list[:]))
+        nc.scalar.activation(picked[:, 3, :], board[3][:].indirect(get_list[:]), COPY)
+
+        hid = [sbuf("hid%d" % h, HALF * PACK, BF16) for h in range(2)]
+        for h in range(2):
+            cols = slice(h * HALF, (h + 1) * HALF)
+            nc.vector.tensor_tensor(
+                hid[h][:].rearrange("p (c e t) -> p c t e", e=4, t=PACK),
+                picked[:, :, cols].rearrange("p t (c e) -> p c t e", e=4),
+                s2_banks[h][:].rearrange("p t (c e) -> p c t e", e=4),
+                MAX,
+            )
+
+        out_rows = out.rearrange("(g p) j -> p g j", p=P)
+        for h in range(2):
+            cols = slice(h * HALF, (h + 1) * HALF)
+            h_words = sbuf("h_words%d" % h, HALF, U32)
+            h_scales = sbuf("h_scales%d" % h, HALF, U8)
+            nc.vector.quantize_mx(out=h_words[:].bitcast(E4M3), scales=h_scales[:], in_=hid[h][:])
+            y_bank = ps.tile([P, 2, HALF], F32, name="y_bank%d" % h)
+            for g in range(2):
+                rows = slice(g * P, (g + 1) * P)
+                nc.tensor.matmul_mx(out=y_bank[:, g, :], lhsT=v_words[:, rows].bitcast(E2M1), lhsT_scale=v_scales[:, rows],
+                                    rhs=h_words[:].bitcast(E4M3), rhs_scale=h_scales[:], start=True, stop=True)
+            y = sb.tile([P, 2, HALF], F32, name="y%d" % h)
+            nc.scalar.copy(y[:], y_bank[:])
+            nc.sync.dma_start(out_rows[:, :, cols], y[:])

@@ -39,14 +39,14 @@ def tile_list_contest_rivals_board_plain_kernel(
             nc.sync.dma_start(tile[:], src)
             return tile
 
-        def load_words(name, src, dtype):
+        def load_words(name, src, dtype, queue=nc.sync):
             tile = sbuf(name, T, dtype)
-            nc.sync.dma_start(tile[:].bitcast(I32), src.bitcast(I32))
+            queue.dma_start(tile[:].bitcast(I32), src.bitcast(I32))
             return tile
 
         def zeroed_plane(name):
             tile = sbuf(name, T, U8)
-            nc.vector.memset(tile[:].bitcast(I32), 0)
+            nc.gpsimd.memset(tile[:].bitcast(I32), 0)
             return tile
 
         def load_scales(queue, tile, src):
@@ -64,19 +64,19 @@ def tile_list_contest_rivals_board_plain_kernel(
             board.append(tile)
 
         q_list = load_list("q_list", offs2)
-        q_table = load_words("q_table", xq_words[0], U16)
+        q_table = load_words("q_table", xq_words[0], U16, nc.scalar)
         k_list = load_list("k_list", offs)
+        load_scales(nc.sync, k_plane, xk_scales)
         k_table = load_words("k_table", xk_words[0].rearrange("p n t -> p (n t)"), U32)
-        load_scales(nc.scalar, k_plane, xk_scales)
-        load_scales(nc.scalar, q_plane, xq_scales)
+        load_scales(nc.sync, q_plane, xq_scales)
         r_list = load_list("r_list", offs3)
-        put_list = load_list("put_list", offs4)
+        v_list = load_list("v_list", offs6)
         r_table = load_words("r_table", xr_words[0].rearrange("p n t -> p (n t)"), U32)
         v_table = load_words("v_table", vs_words[0], U16)
         load_scales(nc.sync, r_plane, xr_scales)
-        v_list = load_list("v_list", offs6)
-        get_list = load_list("get_list", offs5)
+        put_list = load_list("put_list", offs4)
         load_scales(nc.sync, v_plane, vs_scales)
+        get_list = load_list("get_list", offs5)
 
         def gather(name, table, lst, count, dtype):
             tile = sbuf(name, count, dtype)
@@ -97,31 +97,23 @@ def tile_list_contest_rivals_board_plain_kernel(
             cols = slice(t * P, (t + 1) * P)
             return dict(lhsT=k_words[:, cols].bitcast(E4M3), lhsT_scale=k_scales[:, cols])
 
-        s1_bank0 = ps.tile([P, J], F32, name="s1_bank0")
-        s1_bank1 = ps.tile([P, J], F32, name="s1_bank1")
-        s1_bank23 = ps.tile([P, 2 * J], F32, name="s1_bank23")
-        s1_psum = [s1_bank0[:], s1_bank1[:], s1_bank23[:, 0:J], s1_bank23[:, J : 2 * J]]
+        s1_banks = [ps.tile([P, J], F32, name="s1_bank%d" % t) for t in range(PACK)]
         for t in range(PACK):
-            nc.tensor.matmul_mx(out=s1_psum[t], rhs=q_words[:].bitcast(E2M1), rhs_scale=q_scales[:],
+            nc.tensor.matmul_mx(out=s1_banks[t][:], rhs=q_words[:].bitcast(E2M1), rhs_scale=q_scales[:],
                                 start=True, stop=True, **keys(t))
 
-        s1_0 = sbuf("s1_0", J, F32)
-        s1_1 = sbuf("s1_1", J, F32)
-        s1_23 = sbuf("s1_23", 2 * J, F32)
-        picked = sb.tile([P, PACK, J], F32, name="picked", align_bytes=64)
-
-        nc.scalar.copy(s1_0[:], s1_bank0[:])
-        nc.scalar.activation(board[0][:].indirect(put_list[:]), s1_0[:], COPY)
-
         r_words = gather("r_words", r_table, r_list, J, U32)
-        nc.vector.tensor_copy(s1_1[:], s1_bank1[:])
-        nc.vector.tensor_copy(board[1][:].indirect(put_list[:]), s1_1[:])
-
-        nc.scalar.copy(s1_23[:], s1_bank23[:])
-        nc.scalar.activation(board[2][:].indirect(put_list[:]), s1_23[:, 0:J], COPY)
-        nc.scalar.activation(board[3][:].indirect(put_list[:]), s1_23[:, J : 2 * J], COPY)
-
+        v_words = gather("v_words", v_table, v_list, N, U16)
         r_scales = gather("r_scales", r_plane, r_list, J, U8)
+        s1 = [sbuf("s1_%d" % t, J, F32) for t in range(PACK)]
+        for t in range(PACK):
+            nc.scalar.copy(s1[t][:], s1_banks[t][:])
+        for t in (0, 2):
+            nc.vector.tensor_copy(board[t][:].indirect(put_list[:]), s1[t][:])
+        for t in (1, 3):
+            nc.scalar.activation(board[t][:].indirect(put_list[:]), s1[t][:], COPY)
+        v_scales = gather("v_scales", v_plane, v_list, N, U8)
+
         s2_banks = [ps.tile([P, PACK, HALF], F32, name="s2_bank%d" % h) for h in range(2)]
         for h in range(2):
             cols = slice(h * HALF, (h + 1) * HALF)
@@ -129,34 +121,44 @@ def tile_list_contest_rivals_board_plain_kernel(
                 nc.tensor.matmul_mx(out=s2_banks[h][:, t, :], rhs=r_words[:, cols].bitcast(E5M2),
                                     rhs_scale=r_scales[:, cols], start=True, stop=True, **keys(t))
 
-        v_words = gather("v_words", v_table, v_list, N, U16)
-        v_scales = gather("v_scales", v_plane, v_list, N, U8)
-
-        for t in range(3):
-            nc.vector.tensor_copy(picked[:, t, :], board[t][:].indirect(get_list[:]))
-        nc.scalar.activation(picked[:, 3, :], board[3][:].indirect(get_list[:]), COPY)
-
-        hid = [sbuf("hid%d" % h, HALF * PACK, BF16) for h in range(2)]
+        picked = [sb.tile([P, PACK, HALF], F32, name="picked%d" % h, align_bytes=64) for h in range(2)]
         for h in range(2):
-            cols = slice(h * HALF, (h + 1) * HALF)
+            entries = get_list[:, h * HALF // 16 : (h + 1) * HALF // 16]
+            for t in (0, 1, 3, 2):
+                if (h, t) in ((0, 0), (0, 2), (1, 0)):
+                    nc.vector.tensor_copy(picked[h][:, t, :], board[t][:].indirect(entries))
+                else:
+                    nc.scalar.activation(picked[h][:, t, :], board[t][:].indirect(entries), COPY)
+
+        def keep_larger(h, hid):
             nc.vector.tensor_tensor(
-                hid[h][:].rearrange("p (c e t) -> p c t e", e=4, t=PACK),
-                picked[:, :, cols].rearrange("p t (c e) -> p c t e", e=4),
+                hid[:].rearrange("p (c e t) -> p c t e", e=4, t=PACK),
+                picked[h][:].rearrange("p t (c e) -> p c t e", e=4),
                 s2_banks[h][:].rearrange("p t (c e) -> p c t e", e=4),
                 MAX,
             )
 
-        out_rows = out.rearrange("(g p) j -> p g j", p=P)
-        for h in range(2):
-            cols = slice(h * HALF, (h + 1) * HALF)
+        def quantise(h, hid):
             h_words = sbuf("h_words%d" % h, HALF, U32)
             h_scales = sbuf("h_scales%d" % h, HALF, U8)
-            nc.vector.quantize_mx(out=h_words[:].bitcast(E4M3), scales=h_scales[:], in_=hid[h][:])
-            y_bank = ps.tile([P, 2, HALF], F32, name="y_bank%d" % h)
+            nc.vector.quantize_mx(out=h_words[:].bitcast(E4M3), scales=h_scales[:], in_=hid[:])
+            return h_words, h_scales
+
+        out_rows = out.rearrange("(g p) j -> p g j", p=P)
+
+        def product(h, h_words, h_scales, copies):
+            y = sb.tile([P, 2, HALF], F32, name="y%d" % h)
             for g in range(2):
                 rows = slice(g * P, (g + 1) * P)
-                nc.tensor.matmul_mx(out=y_bank[:, g, :], lhsT=v_words[:, rows].bitcast(E2M1), lhsT_scale=v_scales[:, rows],
+                y_bank = ps.tile([P, HALF], F32, name="y_bank%d%d" % (h, g), tag="s1_bank%d" % (2 * h + g))
+                nc.tensor.matmul_mx(out=y_bank[:], lhsT=v_words[:, rows].bitcast(E2M1), lhsT_scale=v_scales[:, rows],
                                     rhs=h_words[:].bitcast(E4M3), rhs_scale=h_scales[:], start=True, stop=True)
-            y = sb.tile([P, 2, HALF], F32, name="y%d" % h)
-            nc.scalar.copy(y[:], y_bank[:])
-            nc.sync.dma_start(out_rows[:, :, cols], y[:])
+                copies[g](y[:, g, :], y_bank[:])
+            nc.sync.dma_start(out_rows[:, :, h * HALF : (h + 1) * HALF], y[:])
+
+        hid = [sbuf("hid%d" % h, HALF * PACK, BF16) for h in range(2)]
+        for h in range(2):
+            keep_larger(h, hid[h])
+        quantised = [quantise(h, hid[h]) for h in range(2)]
+        for h in range(2):
+            product(h, *quantised[h], (nc.scalar.copy, nc.vector.tensor_copy if h else nc.scalar.copy))

from contextlib import ExitStack

import concourse.mybir as mybir

K, T, I, J, N, C = 512, 1024, 512, 256, 256, 512
FLOPS = 2 * K * I * J * 2 + 2 * I * N * J

F32 = mybir.dt.float32
BF16 = mybir.dt.bfloat16
I32 = mybir.dt.int32
U32 = mybir.dt.uint32
U16 = mybir.dt.uint16
U8 = mybir.dt.uint8
E4M3 = mybir.dt.float8_e4m3fn_x4
E5M2 = mybir.dt.float8_e5m2_x4
E2M1 = mybir.dt.float4_e2m1fn_x4
COPY = mybir.ActivationFunctionType.Copy
MAX = mybir.AluOpType.max

P = 128
PACK = 4
HALF = J // 2


def tile_list_contest_rivals_board_plain_kernel(
    tc, xk_words, xk_scales, xq_words, xq_scales, xr_words, xr_scales, vs_words, vs_scales,
    offs, offs2, offs3, offs4, offs5, offs6, out,
):
    nc = tc.nc
    with ExitStack() as ctx:
        sb = ctx.enter_context(tc.tile_pool(name="sb", bufs=1))
        ps = ctx.enter_context(tc.psum_pool(name="ps", bufs=1))

        def sbuf(name, cols, dtype):
            return sb.tile([P, cols], dtype, name=name, align_bytes=64)

        def load_list(name, src):
            tile = sb.tile(list(src.shape), U16, name=name)
            nc.sync.dma_start(tile[:], src)
            return tile

        def load_words(name, src, dtype, queue=nc.sync):
            tile = sbuf(name, T, dtype)
            queue.dma_start(tile[:].bitcast(I32), src.bitcast(I32))
            return tile

        def zeroed_plane(name):
            tile = sbuf(name, T, U8)
            nc.gpsimd.memset(tile[:].bitcast(I32), 0)
            return tile

        def load_scales(queue, tile, src):
            for q in range(4):
                queue.dma_start(tile[32 * q : 32 * q + 4, :].bitcast(I32), src[0, 4 * q : 4 * q + 4, :].bitcast(I32))

        k_plane = zeroed_plane("k_plane")
        q_plane = zeroed_plane("q_plane")
        r_plane = zeroed_plane("r_plane")
        v_plane = zeroed_plane("v_plane")
        board = []
        for t in range(PACK):
            tile = sbuf("board%d" % t, C, F32)
            nc.vector.memset(tile[:], 0.0)
            board.append(tile)

        q_list = load_list("q_list", offs2)
        q_table = load_words("q_table", xq_words[0], U16, nc.scalar)
        k_list = load_list("k_list", offs)
        load_scales(nc.sync, k_plane, xk_scales)
        k_table = load_words("k_table", xk_words[0].rearrange("p n t -> p (n t)"), U32)
        load_scales(nc.sync, q_plane, xq_scales)
        r_list = load_list("r_list", offs3)
        v_list = load_list("v_list", offs6)
        r_table = load_words("r_table", xr_words[0].rearrange("p n t -> p (n t)"), U32)
        v_table = load_words("v_table", vs_words[0], U16)
        load_scales(nc.sync, r_plane, xr_scales)
        put_list = load_list("put_list", offs4)
        load_scales(nc.sync, v_plane, vs_scales)
        get_list = load_list("get_list", offs5)

        def gather(name, table, lst, count, dtype):
            tile = sbuf(name, count, dtype)
            nc.vector.tensor_copy(tile[:], table[:].indirect(lst[:]))
            return tile

        def gather_dealt(name, table, lst, dtype):
            tile = sbuf(name, I, dtype)
            nc.vector.tensor_copy(tile[:].rearrange("p (t m) -> p m t", t=PACK), table[:].indirect(lst[:]))
            return tile

        q_words = gather("q_words", q_table, q_list, J, U16)
        k_scales = gather_dealt("k_scales", k_plane, k_list, U8)
        k_words = gather_dealt("k_words", k_table, k_list, U32)
        q_scales = gather("q_scales", q_plane, q_list, J, U8)

        def keys(t):
            cols = slice(t * P, (t + 1) * P)
            return dict(lhsT=k_words[:, cols].bitcast(E4M3), lhsT_scale=k_scales[:, cols])

        s1_banks = [ps.tile([P, J], F32, name="s1_bank%d" % t) for t in range(PACK)]
        for t in range(PACK):
            nc.tensor.matmul_mx(out=s1_banks[t][:], rhs=q_words[:].bitcast(E2M1), rhs_scale=q_scales[:],
                                start=True, stop=True, **keys(t))

        r_words = gather("r_words", r_table, r_list, J, U32)
        v_words = gather("v_words", v_table, v_list, N, U16)
        r_scales = gather("r_scales", r_plane, r_list, J, U8)
        s1 = [sbuf("s1_%d" % t, J, F32) for t in range(PACK)]
        for t in range(PACK):
            nc.scalar.copy(s1[t][:], s1_banks[t][:])
        for t in (0, 2):
            nc.vector.tensor_copy(board[t][:].indirect(put_list[:]), s1[t][:])
        for t in (1, 3):
            nc.scalar.activation(board[t][:].indirect(put_list[:]), s1[t][:], COPY)
        v_scales = gather("v_scales", v_plane, v_list, N, U8)

        s2_banks = [ps.tile([P, PACK, HALF], F32, name="s2_bank%d" % h) for h in range(2)]
        for h in range(2):
            cols = slice(h * HALF, (h + 1) * HALF)
            for t in range(PACK):
                nc.tensor.matmul_mx(out=s2_banks[h][:, t, :], rhs=r_words[:, cols].bitcast(E5M2),
                                    rhs_scale=r_scales[:, cols], start=True, stop=True, **keys(t))

        picked = [sb.tile([P, PACK, HALF], F32, name="picked%d" % h, align_bytes=64) for h in range(2)]
        for h in range(2):
            entries = get_list[:, h * HALF // 16 : (h + 1) * HALF // 16]
            for t in (0, 1, 3, 2):
                if (h, t) in ((0, 0), (0, 2), (1, 0)):
                    nc.vector.tensor_copy(picked[h][:, t, :], board[t][:].indirect(entries))
                else:
                    nc.scalar.activation(picked[h][:, t, :], board[t][:].indirect(entries), COPY)

        def keep_larger(h, hid):
            nc.vector.tensor_tensor(
                hid[:].rearrange("p (c e t) -> p c t e", e=4, t=PACK),
                picked[h][:].rearrange("p t (c e) -> p c t e", e=4),
                s2_banks[h][:].rearrange("p t (c e) -> p c t e", e=4),
                MAX,
            )

        def quantise(h, hid):
            h_words = sbuf("h_words%d" % h, HALF, U32)
            h_scales = sbuf("h_scales%d" % h, HALF, U8)
            nc.vector.quantize_mx(out=h_words[:].bitcast(E4M3), scales=h_scales[:], in_=hid[:])
            return h_words, h_scales

        out_rows = out.rearrange("(g p) j -> p g j", p=P)

        def product(h, h_words, h_scales, copies):
            y = sb.tile([P, 2, HALF], F32, name="y%d" % h)
            for g in range(2):
                rows = slice(g * P, (g + 1) * P)
                y_bank = ps.tile([P, HALF], F32, name="y_bank%d%d" % (h, g), tag="s1_bank%d" % (2 * h + g))
                nc.tensor.matmul_mx(out=y_bank[:], lhsT=v_words[:, rows].bitcast(E2M1), lhsT_scale=v_scales[:, rows],
                                    rhs=h_words[:].bitcast(E4M3), rhs_scale=h_scales[:], start=True, stop=True)
                copies[g](y[:, g, :], y_bank[:])
            nc.sync.dma_start(out_rows[:, :, h * HALF : (h + 1) * HALF], y[:])

        hid = [sbuf("hid%d" % h, HALF * PACK, BF16) for h in range(2)]
        for h in range(2):
            keep_larger(h, hid[h])
        quantised = [quantise(h, hid[h]) for h in range(2)]
        for h in range(2):
            product(h, *quantised[h], (nc.scalar.copy, nc.vector.tensor_copy if h else nc.scalar.copy))
